import numpy as np
import ml_dtypes


def mxq(x, axis, fmt="e4m3"):
    dtype, down = {"e4m3": (ml_dtypes.float8_e4m3fn, 7), "e5m2": (ml_dtypes.float8_e5m2, 14)}[fmt]
    v = np.moveaxis(np.asarray(x, np.float32).astype(ml_dtypes.bfloat16).astype(np.float64), axis, -1)
    blocks = v.reshape(v.shape[:-1] + (-1, 32))
    amax = np.abs(blocks).max(-1, keepdims=True)
    byte = np.maximum(np.where(amax > 0, np.frexp(amax)[1] - 1 + 127, 0) - down, 1)
    scale = np.exp2(byte - 127.0)
    codes = (blocks / scale).astype(np.float32).astype(dtype).astype(np.float64)
    return np.moveaxis((codes * scale).reshape(v.shape), -1, axis)


WIDE = False


def mx_kscale(k):
    if not WIDE:
        return np.ones(k)
    levels = np.array([10, -10, 5, -5, 0])
    if k % 512:
        return np.exp2(np.random.permutation(np.resize(levels, k // 32))).repeat(32)
    a = np.empty((k // 512, 16))
    for p in range(k // 512):
        a[p, :8] = np.random.permutation(np.resize(levels, 8))
        for g in range(8):
            far = levels[np.abs(levels - a[p, g]) >= 10]
            a[p, g + 8] = far[np.random.randint(len(far))]
    return np.exp2(a.ravel()).repeat(32)


def f64(x):
    return np.asarray(x).astype(np.float64)


def striped(idx):
    return np.tile(idx.reshape(-1, 16).T, (8, 1)).astype(np.uint16)


def unstriped(offs):
    return offs[:16].T.reshape(-1).astype(np.int64)


E2M1 = np.array([0.0, 0.5, 1.0, 1.5, 2.0, 3.0, 4.0, 6.0, -0.0, -0.5, -1.0, -1.5, -2.0, -3.0, -4.0, -6.0])


def pack_weight(w, fmt):
    k, n = w.shape
    w = f64(np.asarray(w, np.float32).astype(ml_dtypes.bfloat16)).reshape(k // 32, 32, n)
    amax = np.abs(w).max(1)
    if fmt == "e4m3":
        byte = np.frexp(amax)[1] - 1 + 127 - 7
    else:
        mant, ex = np.frexp(amax / 6.0)
        byte = np.where(mant > 0.5, ex, ex - 1) + 127
    byte = np.clip(np.where(amax > 0, byte, 1), 1, 254)
    scaled = (w * np.exp2(127.0 - byte)[:, None, :]).reshape(k, n).astype(np.float32)
    by_word = np.ascontiguousarray(scaled.reshape(k // 512, 128, 4, n).transpose(0, 1, 3, 2))
    if fmt == "e4m3":
        words = by_word.astype(ml_dtypes.float8_e4m3fn).view(np.uint8)
    else:
        c = by_word.astype(ml_dtypes.float4_e2m1fn).view(np.uint8) & 0xF
        words = (c[..., 0::2] | (c[..., 1::2] << 4)).reshape(k // 512, 128, 2 * n)
    return np.ascontiguousarray(words), np.ascontiguousarray(byte.astype(np.uint8).reshape(k // 512, 16, n))


def unpack_weight(words, scales, fmt):
    g, _, n = scales.shape
    words = np.ascontiguousarray(words).reshape(g, 128, n, -1)
    if fmt == "e4m3":
        vals = words.view(ml_dtypes.float8_e4m3fn).astype(np.float64)
    else:
        nib = np.empty((g, 128, n, 4), np.uint8)
        nib[..., 0::2] = words & 0xF
        nib[..., 1::2] = words >> 4
        vals = E2M1[nib]
    vals = vals * np.repeat(np.exp2(scales.astype(np.float64) - 127.0), 8, axis=1)[..., None]
    return vals.transpose(0, 1, 3, 2).reshape(g * 512, n)


def gelu(v):
    return 0.5 * v * (1.0 + np.tanh(np.sqrt(2.0 / np.pi) * (v + 0.044715 * v**3)))


K, T, S, H, N = 1024, 2048, 512, 1024, 512

def setup_inputs():
    n = np.random.standard_normal
    s = mx_kscale(K)[:, None]
    u = mx_kscale(H)[:, None]
    tab_words, tab_scales = pack_weight(n((K, T)) * s, "e4m3")
    w1 = 0.54 / np.sqrt(K) * n((K, H)) / s
    w2_words, w2_scales = pack_weight(0.8 / np.sqrt(K) * n((K, H)) / s * u.T, "e2m1")
    w3 = 0.8 / np.sqrt(K) * n((K, H)) / s * u.T
    cong = 1.6 * n((H, S)) * u
    w4_words, w4_scales = pack_weight(n((H, N)) / np.sqrt(H) / u, "e4m3")
    return {
        "tab_words": tab_words, "tab_scales": tab_scales,
        "offs": striped(np.random.permutation(T)[:S]),
        "offs2": striped(np.random.permutation(T)[:S]),
        "offs3": striped(np.random.permutation(T)[:S]),
        "w1": w1.astype(np.float32),
        "w2_words": w2_words, "w2_scales": w2_scales,
        "w3": w3.astype(np.float32),
        "cong": cong.astype(np.float32),
        "w4_words": w4_words, "w4_scales": w4_scales,
    }

def reference(tab_words, tab_scales, offs, offs2, offs3, w1, w2_words, w2_scales, w3, cong, w4_words, w4_scales):
    TW = unpack_weight(tab_words, tab_scales, "e4m3")
    v = TW[:, unstriped(offs)]
    v2 = TW[:, unstriped(offs2)]
    v3 = TW[:, unstriped(offs3)]
    inbound = mxq(f64(w1), 0, "e4m3").T @ v
    door = unpack_weight(w2_words, w2_scales, "e2m1").T @ v2
    outbound = mxq(f64(w3), 0, "e4m3").T @ v3
    h = np.maximum(np.sin(inbound) * f64(cong) + door, outbound)
    y = unpack_weight(w4_words, w4_scales, "e4m3").T @ mxq(h, 0, "e4m3")
    return y

@@ -1,0 +1,252 @@
+from contextlib import ExitStack
+
+import concourse.mybir as mybir
+
+K, T, S, H, N = 1024, 2048, 512, 1024, 512
+FLOPS = 2 * (3 * K * H * S + H * N * S)
+
+F32 = mybir.dt.float32
+BF16 = mybir.dt.bfloat16
+I32 = mybir.dt.int32
+U32 = mybir.dt.uint32
+U16 = mybir.dt.uint16
+U8 = mybir.dt.uint8
+FP8X4 = mybir.dt.float8_e4m3fn_x4
+FP4X4 = mybir.dt.float4_e2m1fn_x4
+ALU = mybir.AluOpType
+ACT = mybir.ActivationFunctionType
+
+P = 128
+PACK = 4
+PASS = P * PACK
+KP = K // PASS
+HP = H // PASS
+CH = 128
+NCH = S // CH
+NT = N // P
+
+
+def tile_list_cross_dock_scores_kernel(tc, tab_words, tab_scales, offs, offs2, offs3, w1, w2_words, w2_scales, w3, cong, w4_words, w4_scales, out):
+    nc = tc.nc
+    with ExitStack() as ctx:
+        lists = ctx.enter_context(tc.tile_pool(name="lists", bufs=1))
+        keep = ctx.enter_context(tc.tile_pool(name="keep", bufs=1))
+        ring = ctx.enter_context(tc.tile_pool(name="ring", bufs=4))
+        psum = ctx.enter_context(tc.psum_pool(name="psum", bufs=1))
+
+        def bank(k, name):
+            return psum.tile([P, 512], F32, name=name, tag="bank%d" % k)
+
+        w2s_raw = keep.tile([P, KP * H], U8, name="w2s_raw", align_bytes=64)
+        tabs = keep.tile([P, T], U8, name="tabs", align_bytes=64)
+        w4s = keep.tile([P, N], U8, name="w4s", align_bytes=64)
+        door_s1 = keep.tile([P, S], U8, name="door_s1", align_bytes=64)
+        nc.vector.memset(tabs[:].bitcast(I32), 0)
+        tabs1 = keep.tile([P, T], U8, name="tabs1", align_bytes=64)
+        nc.vector.memset(tabs1[:].bitcast(I32), 0)
+        nc.vector.memset(w2s_raw[:].bitcast(I32), 0)
+        nc.vector.memset(w4s[:].bitcast(I32), 0)
+
+        tabw = [keep.tile([P, T], I32, name="tabw%d" % a, align_bytes=64) for a in range(KP)]
+
+        def load_tab(a):
+            nc.sync.dma_start(out=tabw[a][:], in_=tab_words[a].rearrange("p t i -> p (t i)").bitcast(I32))
+
+        raw = {}
+
+        def load_w(key, w, a, b, lo, hi):
+            tl = keep.tile([P, PACK, hi - lo], F32, name="raw_%s_%d_%d_%d" % (key, a, b, lo))
+            nc.sync.dma_start(out=tl[:], in_=w[PASS * a:PASS * (a + 1), PASS * b + lo:PASS * b + hi].rearrange("(p j) c -> p j c", j=PACK))
+            raw[key, a, b, lo] = tl
+
+        congs = [keep.tile([P, PACK, S], F32, name="cong%d" % b) for b in range(HP)]
+
+        def load_cong(b):
+            nc.sync.dma_start(out=congs[b][:], in_=cong[PASS * b:PASS * (b + 1), :].rearrange("(p t) j -> p t j", t=PACK))
+
+        load_tab(0)
+        offsets = []
+        for name, src in (("offs", offs), ("offs2", offs2), ("offs3", offs3)):
+            tl = lists.tile([P, S // 16], U16, name=name)
+            nc.sync.dma_start(tl[:], src)
+            offsets.append(tl)
+
+
+        def load_tabs(q):
+            nc.sync.dma_start(out=tabs[32 * q:32 * q + 4 * KP, :].bitcast(I32), in_=tab_scales[:, 4 * q:4 * q + 4, :].bitcast(I32))
+
+        def load_tabs1(q):
+            nc.sync.dma_start(out=tabs1[32 * q:32 * q + 4, :].bitcast(I32), in_=tab_scales[1, 4 * q:4 * q + 4, :].bitcast(I32))
+
+        def load_w2s(q):
+            nc.sync.dma_start(
+                out=w2s_raw[32 * q:32 * q + 4, :].bitcast(I32).rearrange("r (a c) -> r a c", a=KP),
+                in_=w2_scales[:, 4 * q:4 * q + 4, :].bitcast(I32).rearrange("a r c -> r a c"))
+
+        def load_w4s(q):
+            nc.sync.dma_start(out=w4s[32 * q:32 * q + 4 * HP, :].bitcast(I32), in_=w4_scales[:, 4 * q:4 * q + 4, :].bitcast(I32))
+
+        for q in range(4):
+            load_tabs(q)
+        w2_raw = keep.tile([P, KP * 2 * H], U8, name="w2_raw", align_bytes=64)
+        nc.sync.dma_start(out=w2_raw[:].bitcast(I32).rearrange("p (a c) -> p a c", a=KP), in_=w2_words.bitcast(I32).rearrange("a p c -> p a c"))
+        load_w("w1", w1, 0, 0, 0, PASS)
+        for q in range(4):
+            load_tabs1(q)
+        load_w("w1", w1, 1, 0, 0, PASS)
+        load_tab(1)
+        for q in range(4):
+            load_w2s(q)
+        load_cong(0)
+        load_w("w1", w1, 0, 1, 0, PASS)
+        load_w("w1", w1, 1, 1, 0, PASS)
+        load_w("w3", w3, 0, 0, 0, PASS)
+        for q in range(4):
+            load_w4s(q)
+        load_cong(1)
+        load_w("w3", w3, 1, 0, 0, PASS)
+        load_w("w3", w3, 0, 1, 0, PASS)
+        load_w("w3", w3, 1, 1, 0, PASS // 2)
+        load_w("w3", w3, 1, 1, PASS // 2, PASS)
+        w4w = keep.tile([P, HP, N], I32, name="w4w", align_bytes=64)
+        nc.sync.dma_start(out=w4w[:], in_=w4_words.rearrange("a p c i -> p a (c i)").bitcast(I32))
+
+        w2s = keep.tile([P, KP * H], U8, name="w2s", align_bytes=64)
+        w2w = keep.tile([P, KP * 2 * H], U8, name="w2w", align_bytes=64)
+        nc.scalar.copy(out=w2w[:].bitcast(U16).rearrange("p (g t m) -> p g t m", t=PACK, m=P), in_=w2_raw[:].bitcast(U16).rearrange("p (g m t) -> p g t m", t=PACK, m=P))
+
+        gw = [[keep.tile([P, S], U32, name="gw%d_%d" % (l, a), align_bytes=64) for a in range(KP)] for l in range(3)]
+        gs = [keep.tile([P, S], U8, name="gs%d" % l, align_bytes=64) for l in range(3)]
+
+        def gather_words(l, a):
+            nc.vector.tensor_copy(gw[l][a][:], tabw[a][:].bitcast(U32).indirect(offsets[l][:]))
+
+        def gather_scales(l):
+            nc.vector.tensor_copy(gs[l][:], tabs[:].indirect(offsets[l][:]))
+
+        for l in range(3):
+            gather_words(l, 0)
+        for l in range(3):
+            gather_scales(l)
+        nc.vector.tensor_copy(door_s1[:], tabs1[:].indirect(offsets[1][:]))
+
+        staged = {}
+        codes = {}
+        planes = {}
+
+        def cast(key, a, b, lo, hi, copy):
+            if lo == 0:
+                staged[key, a, b] = ring.tile([P, PACK * PASS], BF16, name="staged", align_bytes=64)
+            dst = staged[key, a, b][:].rearrange("p (t m j) -> p m j t", t=PACK, j=PACK)[:, lo // PACK:hi // PACK]
+            copy(out=dst, in_=raw[key, a, b, lo][:].rearrange("p j (m t) -> p m j t", t=PACK))
+
+        def quantise(key, a, b, pieces):
+            codes[key, a, b] = keep.tile([P, PASS], U32, name="codes_%s_%d_%d" % (key, a, b), align_bytes=64)
+            planes[key, a, b] = keep.tile([P, PASS], U8, name="plane_%s_%d_%d" % (key, a, b), align_bytes=64)
+            wd = PASS // pieces
+            for i in range(pieces):
+                nc.vector.quantize_mx(out=codes[key, a, b][:, i * wd:(i + 1) * wd].bitcast(FP8X4), scales=planes[key, a, b][:, i * wd:(i + 1) * wd],
+                                      in_=staged[key, a, b][:, PACK * i * wd:PACK * (i + 1) * wd])
+
+        cast("w1", 0, 0, 0, PASS, nc.scalar.copy)
+        quantise("w1", 0, 0, 1)
+        cast("w1", 1, 0, 0, PASS, nc.scalar.copy)
+        nc.vector.tensor_copy(out=w2s[:].rearrange("p (g t m) -> p g t m", t=PACK, m=P), in_=w2s_raw[:].rearrange("p (g m t) -> p g t m", t=PACK, m=P))
+        for l in range(3):
+            gather_words(l, 1)
+            if l == 0:
+                quantise("w1", 1, 0, 1)
+
+        sines = [keep.tile([P, PACK, S], F32, name="sines%d" % b) for b in range(HP)]
+        prods = [keep.tile([P, PACK, S], F32, name="prods%d" % b) for b in range(HP)]
+        sums = [keep.tile([P, PACK, S], F32, name="sums%d" % b) for b in range(HP)]
+
+        def inbound_side(b):
+            for t in range(PACK):
+                acc = bank(t, "inbound")
+                for a in range(KP):
+                    nc.tensor.matmul_mx(out=acc[:], lhsT=codes["w1", a, b][:, t * P:(t + 1) * P].bitcast(FP8X4), lhsT_scale=planes["w1", a, b][:, t * P:(t + 1) * P],
+                                        rhs=gw[0][a][:].bitcast(FP8X4), rhs_scale=gs[0][4 * a:P, :], start=(a == 0), stop=(a == KP - 1))
+                nc.scalar.activation(out=sines[b][:, t, :], in_=acc[:], func=ACT.Sin)
+            doors = []
+            for t in range(PACK):
+                acc = bank(PACK + t, "door")
+                for a in range(KP):
+                    col = a * H + b * PASS + t * P
+                    nc.tensor.matmul_mx(out=acc[:], lhsT=w2w[:, 2 * col:2 * (col + P)].bitcast(FP4X4), lhsT_scale=w2s[:, col:col + P],
+                                        rhs=gw[1][a][:].bitcast(FP8X4), rhs_scale=(gs[1] if a == 0 else door_s1)[:], start=(a == 0), stop=(a == KP - 1))
+                doors.append(acc)
+            for t in range(0, PACK, 2):
+                nc.vector.tensor_tensor(out=prods[b][:, t:t + 2, :], in0=sines[b][:, t:t + 2, :], in1=congs[b][:, t:t + 2, :], op=ALU.mult)
+            for t in range(PACK):
+                nc.vector.tensor_tensor(out=sums[b][:, t, :], in0=doors[t][:], in1=prods[b][:, t, :], op=ALU.add)
+
+        cast("w1", 0, 1, 0, PASS, nc.scalar.copy)
+        inbound_side(0)
+        quantise("w1", 0, 1, 1)
+        cast("w1", 1, 1, 0, PASS, nc.scalar.copy)
+        quantise("w1", 1, 1, 1)
+        inbound_side(1)
+
+        h_codes = [[keep.tile([P, CH], U32, name="h_codes%d_%d" % (b, c), align_bytes=64) for c in range(NCH)] for b in range(HP)]
+        h_planes = [[keep.tile([P, CH], U8, name="h_plane%d_%d" % (b, c), align_bytes=64) for c in range(NCH)] for b in range(HP)]
+
+        def outbound_pass(accs, a, b):
+            for c in range(NCH):
+                for t in range(PACK):
+                    nc.tensor.matmul_mx(out=accs[c][:, t * CH:(t + 1) * CH], lhsT=codes["w3", a, b][:, t * P:(t + 1) * P].bitcast(FP8X4),
+                                        lhsT_scale=planes["w3", a, b][:, t * P:(t + 1) * P],
+                                        rhs=gw[2][a][:, c * CH:(c + 1) * CH].bitcast(FP8X4), rhs_scale=gs[2][4 * a:P, c * CH:(c + 1) * CH],
+                                        start=(a == 0 and t == 0), stop=(a == KP - 1 and t == PACK - 1))
+
+        def larger(accs, b, c):
+            hb = ring.tile([P, PACK * CH], BF16, name="hb", align_bytes=64)
+            nc.vector.tensor_tensor(out=hb[:].rearrange("p (n i t) -> p n t i", i=2, t=PACK),
+                                    in0=accs[c][:].rearrange("p (t n i) -> p n t i", i=2, t=PACK),
+                                    in1=sums[b][:, :, c * CH:(c + 1) * CH].rearrange("p t (n i) -> p n t i", i=2), op=ALU.max)
+            return hb
+
+        def quantise_h(hb, b, c):
+            nc.vector.quantize_mx(out=h_codes[b][c][:].bitcast(FP8X4), scales=h_planes[b][c][:], in_=hb[:])
+
+        def score_pass(accs, b, c):
+            for nt in range(NT):
+                nc.tensor.matmul_mx(out=accs[c][:, nt * CH:(nt + 1) * CH], lhsT=w4w[:, b, nt * P:(nt + 1) * P].bitcast(FP8X4),
+                                    lhsT_scale=w4s[4 * b:P, nt * P:(nt + 1) * P],
+                                    rhs=h_codes[b][c][:].bitcast(FP8X4), rhs_scale=h_planes[b][c][:],
+                                    start=(b == 0 and nt == 0), stop=(b == HP - 1 and nt == NT - 1))
+
+        def make_h(accs, b, after):
+            waiting = None
+            for c in range(NCH + 1):
+                fresh = larger(accs, b, c) if c < NCH else None
+                if c > 0:
+                    quantise_h(waiting, b, c - 1)
+                    after(c - 1)
+                waiting = fresh
+
+        outs0 = [bank(c, "outbound0") for c in range(NCH)]
+        for a in range(KP):
+            cast("w3", a, 0, 0, PASS, nc.scalar.copy)
+            quantise("w3", a, 0, 1)
+            outbound_pass(outs0, a, 0)
+        cast("w3", 0, 1, 0, PASS, nc.scalar.copy)
+        make_h(outs0, 0, lambda c: None)
+        quantise("w3", 0, 1, 1)
+        outs1 = [bank(NCH + c, "outbound1") for c in range(NCH)]
+        outbound_pass(outs1, 0, 1)
+        cast("w3", 1, 1, 0, PASS // 2, nc.scalar.copy)
+        cast("w3", 1, 1, PASS // 2, PASS, nc.vector.tensor_copy)
+        quantise("w3", 1, 1, PACK)
+        outbound_pass(outs1, 1, 1)
+        scores = [bank(c, "scores") for c in range(NCH)]
+        for c in range(NCH):
+            score_pass(scores, 0, c)
+
+        def finish(c):
+            score_pass(scores, 1, c)
+            res = ring.tile([P, NT, CH], F32, name="res")
+            nc.scalar.copy(out=res[:].rearrange("p nt j -> p (nt j)"), in_=scores[c][:])
+            nc.sync.dma_start(out=out[:, c * CH:(c + 1) * CH].rearrange("(nt p) j -> p nt j", p=P), in_=res[:])
+
+        make_h(outs1, 1, finish)

@@ -19,11 +19,14 @@ ACT = mybir.ActivationFunctionType
 P = 128
 PACK = 4
 PASS = P * PACK
-KP = K // PASS
-HP = H // PASS
-CH = 128
-NCH = S // CH
-NT = N // P
+K_PASSES = K // PASS
+H_PASSES = H // PASS
+QUADRANTS = 4
+CHUNK = 128
+CHUNKS = S // CHUNK
+N_TILES = N // P
+SCALAR_SHARE = 192
+INBOUND, DOOR, OUTBOUND = 0, 1, 2
 
 
 def tile_list_cross_dock_scores_kernel(tc, tab_words, tab_scales, offs, offs2, offs3, w1, w2_words, w2_scales, w3, cong, w4_words, w4_scales, out):
@@ -34,219 +37,234 @@ def tile_list_cross_dock_scores_kernel(tc, tab_words, tab_scales, offs, offs2, o
         ring = ctx.enter_context(tc.tile_pool(name="ring", bufs=4))
         psum = ctx.enter_context(tc.psum_pool(name="psum", bufs=1))
 
-        def bank(k, name):
-            return psum.tile([P, 512], F32, name=name, tag="bank%d" % k)
+        def bank(index, name):
+            return psum.tile([P, PASS], F32, name=name, tag="bank%d" % index)
 
-        w2s_raw = keep.tile([P, KP * H], U8, name="w2s_raw", align_bytes=64)
-        tabs = keep.tile([P, T], U8, name="tabs", align_bytes=64)
-        w4s = keep.tile([P, N], U8, name="w4s", align_bytes=64)
-        door_s1 = keep.tile([P, S], U8, name="door_s1", align_bytes=64)
-        nc.vector.memset(tabs[:].bitcast(I32), 0)
-        tabs1 = keep.tile([P, T], U8, name="tabs1", align_bytes=64)
-        nc.vector.memset(tabs1[:].bitcast(I32), 0)
-        nc.vector.memset(w2s_raw[:].bitcast(I32), 0)
-        nc.vector.memset(w4s[:].bitcast(I32), 0)
+        def mx_tile(columns, dtype, name):
+            return keep.tile([P, columns], dtype, name=name, align_bytes=64)
 
-        tabw = [keep.tile([P, T], I32, name="tabw%d" % a, align_bytes=64) for a in range(KP)]
-
-        def load_tab(a):
-            nc.sync.dma_start(out=tabw[a][:], in_=tab_words[a].rearrange("p t i -> p (t i)").bitcast(I32))
-
+        table_words = [mx_tile(T, I32, "table_words%d" % a) for a in range(K_PASSES)]
+        table_scales = mx_tile(T, U8, "table_scales")
+        door_scales_pass1 = mx_tile(S, U8, "door_scales_pass1")
+        w2_words_raw = mx_tile(K_PASSES * 2 * H, U8, "w2_words_raw")
+        w2_scales_raw = mx_tile(K_PASSES * H, U8, "w2_scales_raw")
+        w4_codes = mx_tile(H_PASSES * N, I32, "w4_codes")
+        w4_planes = mx_tile(N, U8, "w4_planes")
+        offsets = [lists.tile([P, S // 16], U16, name="offsets%d" % i) for i in range(3)]
+        congestion = [keep.tile([P, PACK, S], F32, name="congestion%d" % b) for b in range(H_PASSES)]
         raw = {}
 
-        def load_w(key, w, a, b, lo, hi):
-            tl = keep.tile([P, PACK, hi - lo], F32, name="raw_%s_%d_%d_%d" % (key, a, b, lo))
-            nc.sync.dma_start(out=tl[:], in_=w[PASS * a:PASS * (a + 1), PASS * b + lo:PASS * b + hi].rearrange("(p j) c -> p j c", j=PACK))
-            raw[key, a, b, lo] = tl
+        for filled in (table_scales, w2_scales_raw, door_scales_pass1, w4_planes):
+            nc.vector.memset(filled[:].bitcast(I32), 0)
 
-        congs = [keep.tile([P, PACK, S], F32, name="cong%d" % b) for b in range(HP)]
+        def load_table(a):
+            nc.sync.dma_start(out=table_words[a][:], in_=tab_words[a].rearrange("p t i -> p (t i)").bitcast(I32))
 
-        def load_cong(b):
-            nc.sync.dma_start(out=congs[b][:], in_=cong[PASS * b:PASS * (b + 1), :].rearrange("(p t) j -> p t j", t=PACK))
+        def load_list(i):
+            nc.sync.dma_start(offsets[i][:], (offs, offs2, offs3)[i])
 
-        load_tab(0)
-        offsets = []
-        for name, src in (("offs", offs), ("offs2", offs2), ("offs3", offs3)):
-            tl = lists.tile([P, S // 16], U16, name=name)
-            nc.sync.dma_start(tl[:], src)
-            offsets.append(tl)
+        def load_weight(name, w, a, b):
+            raw[name, a, b] = keep.tile([P, PACK, PASS], F32, name="raw_%s_%d_%d" % (name, a, b))
+            nc.sync.dma_start(out=raw[name, a, b][:], in_=w[PASS * a:PASS * (a + 1), PASS * b:PASS * (b + 1)].rearrange("(p j) c -> p j c", j=PACK))
 
+        def load_congestion(b):
+            nc.sync.dma_start(out=congestion[b][:], in_=cong[PASS * b:PASS * (b + 1), :].rearrange("(p t) j -> p t j", t=PACK))
 
-        def load_tabs(q):
-            nc.sync.dma_start(out=tabs[32 * q:32 * q + 4 * KP, :].bitcast(I32), in_=tab_scales[:, 4 * q:4 * q + 4, :].bitcast(I32))
+        def load_stacked_planes(tile, scales):
+            for q in range(QUADRANTS):
+                nc.sync.dma_start(out=tile[32 * q:32 * q + 8, :].bitcast(I32), in_=scales[:, 4 * q:4 * q + 4, :].bitcast(I32))
 
-        def load_tabs1(q):
-            nc.sync.dma_start(out=tabs1[32 * q:32 * q + 4, :].bitcast(I32), in_=tab_scales[1, 4 * q:4 * q + 4, :].bitcast(I32))
+        def load_w2_scales():
+            for q in range(QUADRANTS):
+                nc.sync.dma_start(
+                    out=w2_scales_raw[32 * q:32 * q + 4, :].bitcast(I32).rearrange("r (a c) -> r a c", a=K_PASSES),
+                    in_=w2_scales[:, 4 * q:4 * q + 4, :].bitcast(I32).rearrange("a r c -> r a c"))
 
-        def load_w2s(q):
-            nc.sync.dma_start(
-                out=w2s_raw[32 * q:32 * q + 4, :].bitcast(I32).rearrange("r (a c) -> r a c", a=KP),
-                in_=w2_scales[:, 4 * q:4 * q + 4, :].bitcast(I32).rearrange("a r c -> r a c"))
+        def load_words(tile, words):
+            nc.sync.dma_start(out=tile[:].bitcast(I32).rearrange("p (a c) -> p a c", a=2), in_=words.bitcast(I32).rearrange("a p c -> p a c"))
 
-        def load_w4s(q):
-            nc.sync.dma_start(out=w4s[32 * q:32 * q + 4 * HP, :].bitcast(I32), in_=w4_scales[:, 4 * q:4 * q + 4, :].bitcast(I32))
+        load_list(INBOUND)
+        load_list(DOOR)
+        load_list(OUTBOUND)
+        load_table(0)
+        load_stacked_planes(table_scales, tab_scales)
+        load_words(w2_words_raw, w2_words)
+        load_weight("w1", w1, 0, 0)
+        load_w2_scales()
+        load_weight("w1", w1, 1, 0)
+        load_table(1)
+        load_weight("w3", w3, 0, 0)
+        load_congestion(0)
 
-        for q in range(4):
-            load_tabs(q)
-        w2_raw = keep.tile([P, KP * 2 * H], U8, name="w2_raw", align_bytes=64)
-        nc.sync.dma_start(out=w2_raw[:].bitcast(I32).rearrange("p (a c) -> p a c", a=KP), in_=w2_words.bitcast(I32).rearrange("a p c -> p a c"))
-        load_w("w1", w1, 0, 0, 0, PASS)
-        for q in range(4):
-            load_tabs1(q)
-        load_w("w1", w1, 1, 0, 0, PASS)
-        load_tab(1)
-        for q in range(4):
-            load_w2s(q)
-        load_cong(0)
-        load_w("w1", w1, 0, 1, 0, PASS)
-        load_w("w1", w1, 1, 1, 0, PASS)
-        load_w("w3", w3, 0, 0, 0, PASS)
-        for q in range(4):
-            load_w4s(q)
-        load_cong(1)
-        load_w("w3", w3, 1, 0, 0, PASS)
-        load_w("w3", w3, 0, 1, 0, PASS)
-        load_w("w3", w3, 1, 1, 0, PASS // 2)
-        load_w("w3", w3, 1, 1, PASS // 2, PASS)
-        w4w = keep.tile([P, HP, N], I32, name="w4w", align_bytes=64)
-        nc.sync.dma_start(out=w4w[:], in_=w4_words.rearrange("a p c i -> p a (c i)").bitcast(I32))
+        picked_words = [[mx_tile(S, U32, "picked_words%d_%d" % (i, a)) for a in range(K_PASSES if i == INBOUND else 1)] for i in range(3)]
+        picked_scales = [mx_tile(S, U8, "picked_scales%d" % i) for i in range(3)]
 
-        w2s = keep.tile([P, KP * H], U8, name="w2s", align_bytes=64)
-        w2w = keep.tile([P, KP * 2 * H], U8, name="w2w", align_bytes=64)
-        nc.scalar.copy(out=w2w[:].bitcast(U16).rearrange("p (g t m) -> p g t m", t=PACK, m=P), in_=w2_raw[:].bitcast(U16).rearrange("p (g m t) -> p g t m", t=PACK, m=P))
+        def gather_words(i, a):
+            nc.vector.tensor_copy(picked_words[i][a][:], table_words[a][:].bitcast(U32).indirect(offsets[i][:]))
 
-        gw = [[keep.tile([P, S], U32, name="gw%d_%d" % (l, a), align_bytes=64) for a in range(KP)] for l in range(3)]
-        gs = [keep.tile([P, S], U8, name="gs%d" % l, align_bytes=64) for l in range(3)]
+        def gather_scales(picked, window, i):
+            nc.vector.tensor_copy(picked[:], window[:].indirect(offsets[i][:]))
 
-        def gather_words(l, a):
-            nc.vector.tensor_copy(gw[l][a][:], tabw[a][:].bitcast(U32).indirect(offsets[l][:]))
+        w2_codes = mx_tile(K_PASSES * 2 * H, U8, "w2_codes")
+        w2_planes = mx_tile(K_PASSES * H, U8, "w2_planes")
 
-        def gather_scales(l):
-            nc.vector.tensor_copy(gs[l][:], tabs[:].indirect(offsets[l][:]))
+        def deal(copy, dealt, loaded):
+            copy(out=dealt.rearrange("p (g t m) -> p g t m", t=PACK, m=P), in_=loaded.rearrange("p (g m t) -> p g t m", t=PACK, m=P))
 
-        for l in range(3):
-            gather_words(l, 0)
-        for l in range(3):
-            gather_scales(l)
-        nc.vector.tensor_copy(door_s1[:], tabs1[:].indirect(offsets[1][:]))
+        rounded, codes, planes = {}, {}, {}
 
-        staged = {}
-        codes = {}
-        planes = {}
+        def buffer_of(kind, name, a, b):
+            if (kind, name, a, b) in (("codes", "w1", 1, 1), ("rounded", "w3", 1, 1)):
+                return "last", 1
+            if (kind != "rounded" and (name, a, b) == ("w1", 1, 0)) or (kind == "rounded" and (name, b) != ("w1", 0)):
+                return "pair", 2
+            return "%s_%s_%d_%d" % (kind, name, a, b), 1
 
-        def cast(key, a, b, lo, hi, copy):
-            if lo == 0:
-                staged[key, a, b] = ring.tile([P, PACK * PASS], BF16, name="staged", align_bytes=64)
-            dst = staged[key, a, b][:].rearrange("p (t m j) -> p m j t", t=PACK, j=PACK)[:, lo // PACK:hi // PACK]
-            copy(out=dst, in_=raw[key, a, b, lo][:].rearrange("p j (m t) -> p m j t", t=PACK))
+        def round_weight(name, a, b, shares):
+            tag, bufs = buffer_of("rounded", name, a, b)
+            rounded[name, a, b] = keep.tile([P, PACK * PASS], BF16, name="rounded_%s_%d_%d" % (name, a, b), tag=tag, bufs=bufs, align_bytes=64)
+            for copy, first, last in shares:
+                copy(out=rounded[name, a, b][:].rearrange("p (t m j) -> p m j t", t=PACK, j=PACK)[:, first // PACK:last // PACK],
+                     in_=raw[name, a, b][:, :, first:last].rearrange("p j (m t) -> p m j t", t=PACK))
 
-        def quantise(key, a, b, pieces):
-            codes[key, a, b] = keep.tile([P, PASS], U32, name="codes_%s_%d_%d" % (key, a, b), align_bytes=64)
-            planes[key, a, b] = keep.tile([P, PASS], U8, name="plane_%s_%d_%d" % (key, a, b), align_bytes=64)
-            wd = PASS // pieces
-            for i in range(pieces):
-                nc.vector.quantize_mx(out=codes[key, a, b][:, i * wd:(i + 1) * wd].bitcast(FP8X4), scales=planes[key, a, b][:, i * wd:(i + 1) * wd],
-                                      in_=staged[key, a, b][:, PACK * i * wd:PACK * (i + 1) * wd])
+        on_scalar = [(nc.scalar.copy, 0, PASS)]
+        on_vector = [(nc.vector.tensor_copy, 0, PASS)]
+        on_both = [(nc.scalar.copy, 0, SCALAR_SHARE), (nc.vector.tensor_copy, SCALAR_SHARE, PASS)]
 
-        cast("w1", 0, 0, 0, PASS, nc.scalar.copy)
-        quantise("w1", 0, 0, 1)
-        cast("w1", 1, 0, 0, PASS, nc.scalar.copy)
-        nc.vector.tensor_copy(out=w2s[:].rearrange("p (g t m) -> p g t m", t=PACK, m=P), in_=w2s_raw[:].rearrange("p (g m t) -> p g t m", t=PACK, m=P))
-        for l in range(3):
-            gather_words(l, 1)
-            if l == 0:
-                quantise("w1", 1, 0, 1)
+        def quantise_weight(name, a, b, pieces):
+            tag, bufs = buffer_of("codes", name, a, b)
+            codes[name, a, b] = keep.tile([P, PASS], U32, name="codes_%s_%d_%d" % (name, a, b), tag=tag, bufs=bufs, align_bytes=64)
+            tag, bufs = buffer_of("plane", name, a, b)
+            planes[name, a, b] = keep.tile([P, PASS], U8, name="plane_%s_%d_%d" % (name, a, b), tag=tag, bufs=bufs, align_bytes=64)
+            width = PASS // pieces
+            for first in range(0, PASS, width):
+                nc.vector.quantize_mx(out=codes[name, a, b][:, first:first + width].bitcast(FP8X4), scales=planes[name, a, b][:, first:first + width],
+                                      in_=rounded[name, a, b][:, PACK * first:PACK * (first + width)])
 
-        sines = [keep.tile([P, PACK, S], F32, name="sines%d" % b) for b in range(HP)]
-        prods = [keep.tile([P, PACK, S], F32, name="prods%d" % b) for b in range(HP)]
-        sums = [keep.tile([P, PACK, S], F32, name="sums%d" % b) for b in range(HP)]
+        sines, products = {}, {}
+        sums = [keep.tile([P, PACK, S], F32, name="sums%d" % b) for b in range(H_PASSES)]
 
-        def inbound_side(b):
+        def inbound_sines(b):
+            sines[b] = keep.tile([P, PACK, S], F32, name="sines")
             for t in range(PACK):
-                acc = bank(t, "inbound")
-                for a in range(KP):
+                acc = bank(PACK * b + t, "inbound")
+                for a in range(K_PASSES):
                     nc.tensor.matmul_mx(out=acc[:], lhsT=codes["w1", a, b][:, t * P:(t + 1) * P].bitcast(FP8X4), lhsT_scale=planes["w1", a, b][:, t * P:(t + 1) * P],
-                                        rhs=gw[0][a][:].bitcast(FP8X4), rhs_scale=gs[0][4 * a:P, :], start=(a == 0), stop=(a == KP - 1))
+                                        rhs=picked_words[INBOUND][a][:].bitcast(FP8X4), rhs_scale=picked_scales[INBOUND][4 * a:P, :],
+                                        start=(a == 0), stop=(a == K_PASSES - 1))
                 nc.scalar.activation(out=sines[b][:, t, :], in_=acc[:], func=ACT.Sin)
+
+        def door_sums(b):
+            products[b] = keep.tile([P, PACK, S], F32, name="products")
             doors = []
             for t in range(PACK):
                 acc = bank(PACK + t, "door")
-                for a in range(KP):
-                    col = a * H + b * PASS + t * P
-                    nc.tensor.matmul_mx(out=acc[:], lhsT=w2w[:, 2 * col:2 * (col + P)].bitcast(FP4X4), lhsT_scale=w2s[:, col:col + P],
-                                        rhs=gw[1][a][:].bitcast(FP8X4), rhs_scale=(gs[1] if a == 0 else door_s1)[:], start=(a == 0), stop=(a == KP - 1))
+                for a in range(K_PASSES):
+                    column = a * H + b * PASS + t * P
+                    nc.tensor.matmul_mx(out=acc[:], lhsT=w2_codes[:, 2 * column:2 * (column + P)].bitcast(FP4X4), lhsT_scale=w2_planes[:, column:column + P],
+                                        rhs=picked_words[DOOR][a][:].bitcast(FP8X4), rhs_scale=(picked_scales[DOOR], door_scales_pass1)[a][:],
+                                        start=(a == 0), stop=(a == K_PASSES - 1))
                 doors.append(acc)
-            for t in range(0, PACK, 2):
-                nc.vector.tensor_tensor(out=prods[b][:, t:t + 2, :], in0=sines[b][:, t:t + 2, :], in1=congs[b][:, t:t + 2, :], op=ALU.mult)
+            for first, last in ((0, 1), (1, 2), (2, 4)):
+                nc.vector.tensor_tensor(out=products[b][:, first:last, :], in0=sines[b][:, first:last, :], in1=congestion[b][:, first:last, :], op=ALU.mult)
             for t in range(PACK):
-                nc.vector.tensor_tensor(out=sums[b][:, t, :], in0=doors[t][:], in1=prods[b][:, t, :], op=ALU.add)
-
-        cast("w1", 0, 1, 0, PASS, nc.scalar.copy)
-        inbound_side(0)
-        quantise("w1", 0, 1, 1)
-        cast("w1", 1, 1, 0, PASS, nc.scalar.copy)
-        quantise("w1", 1, 1, 1)
-        inbound_side(1)
-
-        h_codes = [[keep.tile([P, CH], U32, name="h_codes%d_%d" % (b, c), align_bytes=64) for c in range(NCH)] for b in range(HP)]
-        h_planes = [[keep.tile([P, CH], U8, name="h_plane%d_%d" % (b, c), align_bytes=64) for c in range(NCH)] for b in range(HP)]
+                nc.vector.tensor_tensor(out=sums[b][:, t, :], in0=doors[t][:], in1=products[b][:, t, :], op=ALU.add)
 
         def outbound_pass(accs, a, b):
-            for c in range(NCH):
+            for c in range(CHUNKS):
+                entries = slice(c * CHUNK, (c + 1) * CHUNK)
                 for t in range(PACK):
-                    nc.tensor.matmul_mx(out=accs[c][:, t * CH:(t + 1) * CH], lhsT=codes["w3", a, b][:, t * P:(t + 1) * P].bitcast(FP8X4),
+                    nc.tensor.matmul_mx(out=accs[c][:, t * CHUNK:(t + 1) * CHUNK], lhsT=codes["w3", a, b][:, t * P:(t + 1) * P].bitcast(FP8X4),
                                         lhsT_scale=planes["w3", a, b][:, t * P:(t + 1) * P],
-                                        rhs=gw[2][a][:, c * CH:(c + 1) * CH].bitcast(FP8X4), rhs_scale=gs[2][4 * a:P, c * CH:(c + 1) * CH],
-                                        start=(a == 0 and t == 0), stop=(a == KP - 1 and t == PACK - 1))
+                                        rhs=picked_words[OUTBOUND][a][:, entries].bitcast(FP8X4), rhs_scale=picked_scales[OUTBOUND][4 * a:P, entries],
+                                        start=(a == 0 and t == 0), stop=(a == K_PASSES - 1 and t == PACK - 1))
 
-        def larger(accs, b, c):
-            hb = ring.tile([P, PACK * CH], BF16, name="hb", align_bytes=64)
-            nc.vector.tensor_tensor(out=hb[:].rearrange("p (n i t) -> p n t i", i=2, t=PACK),
+        h_rounded = [mx_tile(PACK * S, BF16, "h_rounded%d" % b) for b in range(H_PASSES)]
+        h_codes = [mx_tile(S, U32, "h_codes%d" % b) for b in range(H_PASSES)]
+        h_planes = [mx_tile(S, U8, "h_plane%d" % b) for b in range(H_PASSES)]
+
+        def larger_side(accs, b, c):
+            nc.vector.tensor_tensor(out=h_rounded[b][:, PACK * c * CHUNK:PACK * (c + 1) * CHUNK].rearrange("p (n i t) -> p n t i", i=2, t=PACK),
                                     in0=accs[c][:].rearrange("p (t n i) -> p n t i", i=2, t=PACK),
-                                    in1=sums[b][:, :, c * CH:(c + 1) * CH].rearrange("p t (n i) -> p n t i", i=2), op=ALU.max)
-            return hb
+                                    in1=sums[b][:, :, c * CHUNK:(c + 1) * CHUNK].rearrange("p t (n i) -> p n t i", i=2), op=ALU.max)
 
-        def quantise_h(hb, b, c):
-            nc.vector.quantize_mx(out=h_codes[b][c][:].bitcast(FP8X4), scales=h_planes[b][c][:], in_=hb[:])
+        def quantise_h(b, first, last):
+            nc.vector.quantize_mx(out=h_codes[b][:, first:last].bitcast(FP8X4), scales=h_planes[b][:, first:last], in_=h_rounded[b][:, PACK * first:PACK * last])
 
-        def score_pass(accs, b, c):
-            for nt in range(NT):
-                nc.tensor.matmul_mx(out=accs[c][:, nt * CH:(nt + 1) * CH], lhsT=w4w[:, b, nt * P:(nt + 1) * P].bitcast(FP8X4),
-                                    lhsT_scale=w4s[4 * b:P, nt * P:(nt + 1) * P],
-                                    rhs=h_codes[b][c][:].bitcast(FP8X4), rhs_scale=h_planes[b][c][:],
-                                    start=(b == 0 and nt == 0), stop=(b == HP - 1 and nt == NT - 1))
+        def score_pass(targets, b, c):
+            entries = slice(c * CHUNK, (c + 1) * CHUNK)
+            for acc, tiles in targets:
+                for place, nt in enumerate(tiles):
+                    nc.tensor.matmul_mx(out=acc[:, place * CHUNK:(place + 1) * CHUNK], lhsT=w4_codes[:, b * N + nt * P:b * N + (nt + 1) * P].bitcast(FP8X4),
+                                        lhsT_scale=w4_planes[4 * b:P, nt * P:(nt + 1) * P],
+                                        rhs=h_codes[b][:, entries].bitcast(FP8X4), rhs_scale=h_planes[b][:, entries],
+                                        start=(b == 0 and place == 0), stop=(b == H_PASSES - 1 and place == len(tiles) - 1))
 
-        def make_h(accs, b, after):
-            waiting = None
-            for c in range(NCH + 1):
-                fresh = larger(accs, b, c) if c < NCH else None
-                if c > 0:
-                    quantise_h(waiting, b, c - 1)
-                    after(c - 1)
-                waiting = fresh
+        def store_scores(acc, tiles, c, copy, queue):
+            result = ring.tile([P, len(tiles), CHUNK], F32, name="result", bufs=5)
+            copy(out=result[:].rearrange("p nt j -> p (nt j)"), in_=acc[:, :len(tiles) * CHUNK])
+            queue.dma_start(out=out[tiles[0] * P:(tiles[-1] + 1) * P, c * CHUNK:(c + 1) * CHUNK].rearrange("(nt p) j -> p nt j", p=P), in_=result[:])
 
-        outs0 = [bank(c, "outbound0") for c in range(NCH)]
-        for a in range(KP):
-            cast("w3", a, 0, 0, PASS, nc.scalar.copy)
-            quantise("w3", a, 0, 1)
-            outbound_pass(outs0, a, 0)
-        cast("w3", 0, 1, 0, PASS, nc.scalar.copy)
-        make_h(outs0, 0, lambda c: None)
-        quantise("w3", 0, 1, 1)
-        outs1 = [bank(NCH + c, "outbound1") for c in range(NCH)]
-        outbound_pass(outs1, 0, 1)
-        cast("w3", 1, 1, 0, PASS // 2, nc.scalar.copy)
-        cast("w3", 1, 1, PASS // 2, PASS, nc.vector.tensor_copy)
-        quantise("w3", 1, 1, PACK)
-        outbound_pass(outs1, 1, 1)
-        scores = [bank(c, "scores") for c in range(NCH)]
-        for c in range(NCH):
-            score_pass(scores, 0, c)
-
-        def finish(c):
-            score_pass(scores, 1, c)
-            res = ring.tile([P, NT, CH], F32, name="res")
-            nc.scalar.copy(out=res[:].rearrange("p nt j -> p (nt j)"), in_=scores[c][:])
-            nc.sync.dma_start(out=out[:, c * CH:(c + 1) * CH].rearrange("(nt p) j -> p nt j", p=P), in_=res[:])
-
-        make_h(outs1, 1, finish)
+        gather_scales(picked_scales[DOOR], table_scales, DOOR)
+        nc.sync.dma_start(out=door_scales_pass1[0:P - 4, :].bitcast(I32), in_=picked_scales[DOOR][4:P, :].bitcast(I32))
+        load_weight("w3", w3, 1, 0)
+        load_weight("w1", w1, 0, 1)
+        load_weight("w1", w1, 1, 1)
+        load_weight("w3", w3, 0, 1)
+        load_congestion(1)
+        load_stacked_planes(w4_planes, w4_scales)
+        load_weight("w3", w3, 1, 1)
+        load_words(w4_codes, w4_words.rearrange("a p c i -> a p (c i)"))
+        gather_words(INBOUND, 0)
+        gather_words(DOOR, 0)
+        gather_words(OUTBOUND, 0)
+        gather_scales(picked_scales[INBOUND], table_scales, INBOUND)
+        gather_scales(picked_scales[OUTBOUND], table_scales, OUTBOUND)
+        deal(nc.scalar.copy, w2_codes[:].bitcast(U16), w2_words_raw[:].bitcast(U16))
+        deal(nc.vector.tensor_copy, w2_planes[:], w2_scales_raw[:])
+        round_weight("w1", 0, 0, on_scalar)
+        quantise_weight("w1", 0, 0, 1)
+        round_weight("w1", 1, 0, on_scalar)
+        quantise_weight("w1", 1, 0, 1)
+        gather_words(INBOUND, 1)
+        inbound_sines(0)
+        late_words = keep.tile([P, 2 * S], U32, name="late_words", tag="rounded_w1_1_0", align_bytes=64)
+        picked_words[DOOR].append(late_words[:, :S])
+        picked_words[OUTBOUND].append(late_words[:, S:])
+        gather_words(DOOR, 1)
+        gather_words(OUTBOUND, 1)
+        round_weight("w3", 0, 0, on_scalar)
+        quantise_weight("w3", 0, 0, 1)
+        outbound = [bank(c, "outbound") for c in range(CHUNKS)]
+        outbound_pass(outbound, 0, 0)
+        round_weight("w3", 1, 0, on_scalar)
+        quantise_weight("w3", 1, 0, 1)
+        outbound_pass(outbound, 1, 0)
+        door_sums(0)
+        round_weight("w1", 0, 1, on_scalar)
+        quantise_weight("w1", 0, 1, 1)
+        round_weight("w1", 1, 1, on_vector)
+        quantise_weight("w1", 1, 1, 1)
+        inbound_sines(1)
+        for c in range(CHUNKS):
+            larger_side(outbound, 0, c)
+        quantise_h(0, 0, S)
+        round_weight("w3", 0, 1, on_scalar)
+        quantise_weight("w3", 0, 1, 1)
+        outbound = [bank(c, "outbound") for c in range(CHUNKS)]
+        outbound_pass(outbound, 0, 1)
+        door_sums(1)
+        round_weight("w3", 1, 1, on_scalar)
+        quantise_weight("w3", 1, 1, 2)
+        outbound_pass(outbound, 1, 1)
+        every = list(range(N_TILES))
+        targets = [[(bank(CHUNKS + c, "scores"), every)] for c in range(CHUNKS)]
+        for c in range(CHUNKS):
+            score_pass(targets[c], 0, c)
+        larger_side(outbound, 1, 0)
+        for c in range(CHUNKS):
+            if c + 1 < CHUNKS:
+                larger_side(outbound, 1, c + 1)
+            quantise_h(1, c * CHUNK, (c + 1) * CHUNK)
+            score_pass(targets[c], 1, c)
+            store_scores(targets[c][0][0], every, c, nc.scalar.copy, nc.sync)

@@ -64,7 +64,8 @@ def tile_list_cross_dock_scores_kernel(tc, tab_words, tab_scales, offs, offs2, o
             nc.sync.dma_start(offsets[i][:], (offs, offs2, offs3)[i])
 
         def load_weight(name, w, a, b):
-            raw[name, a, b] = keep.tile([P, PACK, PASS], F32, name="raw_%s_%d_%d" % (name, a, b))
+            tag = "raw_%s_%d_%d" % (name, a, b)
+            raw[name, a, b] = keep.tile([P, PACK, PASS], F32, name="raw_%s_%d_%d" % (name, a, b), tag=tag, align_bytes=64)
             nc.sync.dma_start(out=raw[name, a, b][:], in_=w[PASS * a:PASS * (a + 1), PASS * b:PASS * (b + 1)].rearrange("(p j) c -> p j c", j=PACK))
 
         def load_congestion(b):
@@ -113,12 +114,15 @@ def tile_list_cross_dock_scores_kernel(tc, tab_words, tab_scales, offs, offs2, o
 
         rounded, codes, planes = {}, {}, {}
 
+        shared = {
+            ("plane", "w1", 1, 0): "first", ("rounded", "w1", 0, 1): "first",
+            ("codes", "w1", 1, 0): "second", ("rounded", "w3", 1, 0): "second", ("rounded", "w1", 1, 1): "second",
+            ("rounded", "w3", 0, 0): "third", ("rounded", "w3", 0, 1): "third",
+            ("codes", "w1", 1, 1): "last", ("rounded", "w3", 1, 1): "last",
+        }
+
         def buffer_of(kind, name, a, b):
-            if (kind, name, a, b) in (("codes", "w1", 1, 1), ("rounded", "w3", 1, 1)):
-                return "last", 1
-            if (kind != "rounded" and (name, a, b) == ("w1", 1, 0)) or (kind == "rounded" and (name, b) != ("w1", 0)):
-                return "pair", 2
-            return "%s_%s_%d_%d" % (kind, name, a, b), 1
+            return shared.get((kind, name, a, b), "%s_%s_%d_%d" % (kind, name, a, b)), 1
 
         def round_weight(name, a, b, shares):
             tag, bufs = buffer_of("rounded", name, a, b)
@@ -179,7 +183,7 @@ def tile_list_cross_dock_scores_kernel(tc, tab_words, tab_scales, offs, offs2, o
                                         rhs=picked_words[OUTBOUND][a][:, entries].bitcast(FP8X4), rhs_scale=picked_scales[OUTBOUND][4 * a:P, entries],
                                         start=(a == 0 and t == 0), stop=(a == K_PASSES - 1 and t == PACK - 1))
 
-        h_rounded = [mx_tile(PACK * S, BF16, "h_rounded%d" % b) for b in range(H_PASSES)]
+        h_rounded = {}
         h_codes = [mx_tile(S, U32, "h_codes%d" % b) for b in range(H_PASSES)]
         h_planes = [mx_tile(S, U8, "h_plane%d" % b) for b in range(H_PASSES)]
 
@@ -242,14 +246,15 @@ def tile_list_cross_dock_scores_kernel(tc, tab_words, tab_scales, offs, offs2, o
         outbound_pass(outbound, 1, 0)
         door_sums(0)
         round_weight("w1", 0, 1, on_scalar)
-        quantise_weight("w1", 0, 1, 1)
+        round_weight("w3", 0, 1, on_scalar)
         round_weight("w1", 1, 1, on_vector)
         quantise_weight("w1", 1, 1, 1)
+        quantise_weight("w1", 0, 1, 1)
         inbound_sines(1)
+        h_rounded[0] = keep.tile([P, PACK * S], BF16, name="h_rounded0", tag="first", align_bytes=64)
         for c in range(CHUNKS):
             larger_side(outbound, 0, c)
         quantise_h(0, 0, S)
-        round_weight("w3", 0, 1, on_scalar)
         quantise_weight("w3", 0, 1, 1)
         outbound = [bank(c, "outbound") for c in range(CHUNKS)]
         outbound_pass(outbound, 0, 1)
@@ -257,6 +262,7 @@ def tile_list_cross_dock_scores_kernel(tc, tab_words, tab_scales, offs, offs2, o
         round_weight("w3", 1, 1, on_scalar)
         quantise_weight("w3", 1, 1, 2)
         outbound_pass(outbound, 1, 1)
+        h_rounded[1] = mx_tile(PACK * S, BF16, "h_rounded1")
         every = list(range(N_TILES))
         targets = [[(bank(CHUNKS + c, "scores"), every)] for c in range(CHUNKS)]
         for c in range(CHUNKS):

from contextlib import ExitStack

import concourse.mybir as mybir

K, T, S, H, N = 1024, 2048, 512, 1024, 512
FLOPS = 2 * (3 * K * H * S + H * N * S)

F32 = mybir.dt.float32
BF16 = mybir.dt.bfloat16
I32 = mybir.dt.int32
U32 = mybir.dt.uint32
U16 = mybir.dt.uint16
U8 = mybir.dt.uint8
FP8X4 = mybir.dt.float8_e4m3fn_x4
FP4X4 = mybir.dt.float4_e2m1fn_x4
ALU = mybir.AluOpType
ACT = mybir.ActivationFunctionType

P = 128
PACK = 4
PASS = P * PACK
K_PASSES = K // PASS
H_PASSES = H // PASS
QUADRANTS = 4
CHUNK = 128
CHUNKS = S // CHUNK
N_TILES = N // P
SCALAR_SHARE = 192
INBOUND, DOOR, OUTBOUND = 0, 1, 2


def tile_list_cross_dock_scores_kernel(tc, tab_words, tab_scales, offs, offs2, offs3, w1, w2_words, w2_scales, w3, cong, w4_words, w4_scales, out):
    nc = tc.nc
    with ExitStack() as ctx:
        lists = ctx.enter_context(tc.tile_pool(name="lists", bufs=1))
        keep = ctx.enter_context(tc.tile_pool(name="keep", bufs=1))
        ring = ctx.enter_context(tc.tile_pool(name="ring", bufs=4))
        psum = ctx.enter_context(tc.psum_pool(name="psum", bufs=1))

        def bank(index, name):
            return psum.tile([P, PASS], F32, name=name, tag="bank%d" % index)

        def mx_tile(columns, dtype, name):
            return keep.tile([P, columns], dtype, name=name, align_bytes=64)

        table_words = [mx_tile(T, I32, "table_words%d" % a) for a in range(K_PASSES)]
        table_scales = mx_tile(T, U8, "table_scales")
        door_scales_pass1 = mx_tile(S, U8, "door_scales_pass1")
        w2_words_raw = mx_tile(K_PASSES * 2 * H, U8, "w2_words_raw")
        w2_scales_raw = mx_tile(K_PASSES * H, U8, "w2_scales_raw")
        w4_codes = mx_tile(H_PASSES * N, I32, "w4_codes")
        w4_planes = mx_tile(N, U8, "w4_planes")
        offsets = [lists.tile([P, S // 16], U16, name="offsets%d" % i) for i in range(3)]
        congestion = [keep.tile([P, PACK, S], F32, name="congestion%d" % b) for b in range(H_PASSES)]
        raw = {}

        for filled in (table_scales, w2_scales_raw, door_scales_pass1, w4_planes):
            nc.vector.memset(filled[:].bitcast(I32), 0)

        def load_table(a):
            nc.sync.dma_start(out=table_words[a][:], in_=tab_words[a].rearrange("p t i -> p (t i)").bitcast(I32))

        def load_list(i):
            nc.sync.dma_start(offsets[i][:], (offs, offs2, offs3)[i])

        def load_weight(name, w, a, b):
            tag = "raw_%s_%d_%d" % (name, a, b)
            raw[name, a, b] = keep.tile([P, PACK, PASS], F32, name="raw_%s_%d_%d" % (name, a, b), tag=tag, align_bytes=64)
            nc.sync.dma_start(out=raw[name, a, b][:], in_=w[PASS * a:PASS * (a + 1), PASS * b:PASS * (b + 1)].rearrange("(p j) c -> p j c", j=PACK))

        def load_congestion(b):
            nc.sync.dma_start(out=congestion[b][:], in_=cong[PASS * b:PASS * (b + 1), :].rearrange("(p t) j -> p t j", t=PACK))

        def load_stacked_planes(tile, scales):
            for q in range(QUADRANTS):
                nc.sync.dma_start(out=tile[32 * q:32 * q + 8, :].bitcast(I32), in_=scales[:, 4 * q:4 * q + 4, :].bitcast(I32))

        def load_w2_scales():
            for q in range(QUADRANTS):
                nc.sync.dma_start(
                    out=w2_scales_raw[32 * q:32 * q + 4, :].bitcast(I32).rearrange("r (a c) -> r a c", a=K_PASSES),
                    in_=w2_scales[:, 4 * q:4 * q + 4, :].bitcast(I32).rearrange("a r c -> r a c"))

        def load_words(tile, words):
            nc.sync.dma_start(out=tile[:].bitcast(I32).rearrange("p (a c) -> p a c", a=2), in_=words.bitcast(I32).rearrange("a p c -> p a c"))

        load_list(INBOUND)
        load_list(DOOR)
        load_list(OUTBOUND)
        load_table(0)
        load_stacked_planes(table_scales, tab_scales)
        load_words(w2_words_raw, w2_words)
        load_weight("w1", w1, 0, 0)
        load_w2_scales()
        load_weight("w1", w1, 1, 0)
        load_table(1)
        load_weight("w3", w3, 0, 0)
        load_congestion(0)

        picked_words = [[mx_tile(S, U32, "picked_words%d_%d" % (i, a)) for a in range(K_PASSES if i == INBOUND else 1)] for i in range(3)]
        picked_scales = [mx_tile(S, U8, "picked_scales%d" % i) for i in range(3)]

        def gather_words(i, a):
            nc.vector.tensor_copy(picked_words[i][a][:], table_words[a][:].bitcast(U32).indirect(offsets[i][:]))

        def gather_scales(picked, window, i):
            nc.vector.tensor_copy(picked[:], window[:].indirect(offsets[i][:]))

        w2_codes = mx_tile(K_PASSES * 2 * H, U8, "w2_codes")
        w2_planes = mx_tile(K_PASSES * H, U8, "w2_planes")

        def deal(copy, dealt, loaded):
            copy(out=dealt.rearrange("p (g t m) -> p g t m", t=PACK, m=P), in_=loaded.rearrange("p (g m t) -> p g t m", t=PACK, m=P))

        rounded, codes, planes = {}, {}, {}

        shared = {
            ("plane", "w1", 1, 0): "first", ("rounded", "w1", 0, 1): "first",
            ("codes", "w1", 1, 0): "second", ("rounded", "w3", 1, 0): "second", ("rounded", "w1", 1, 1): "second",
            ("rounded", "w3", 0, 0): "third", ("rounded", "w3", 0, 1): "third",
            ("codes", "w1", 1, 1): "last", ("rounded", "w3", 1, 1): "last",
        }

        def buffer_of(kind, name, a, b):
            return shared.get((kind, name, a, b), "%s_%s_%d_%d" % (kind, name, a, b)), 1

        def round_weight(name, a, b, shares):
            tag, bufs = buffer_of("rounded", name, a, b)
            rounded[name, a, b] = keep.tile([P, PACK * PASS], BF16, name="rounded_%s_%d_%d" % (name, a, b), tag=tag, bufs=bufs, align_bytes=64)
            for copy, first, last in shares:
                copy(out=rounded[name, a, b][:].rearrange("p (t m j) -> p m j t", t=PACK, j=PACK)[:, first // PACK:last // PACK],
                     in_=raw[name, a, b][:, :, first:last].rearrange("p j (m t) -> p m j t", t=PACK))

        on_scalar = [(nc.scalar.copy, 0, PASS)]
        on_vector = [(nc.vector.tensor_copy, 0, PASS)]
        on_both = [(nc.scalar.copy, 0, SCALAR_SHARE), (nc.vector.tensor_copy, SCALAR_SHARE, PASS)]

        def quantise_weight(name, a, b, pieces):
            tag, bufs = buffer_of("codes", name, a, b)
            codes[name, a, b] = keep.tile([P, PASS], U32, name="codes_%s_%d_%d" % (name, a, b), tag=tag, bufs=bufs, align_bytes=64)
            tag, bufs = buffer_of("plane", name, a, b)
            planes[name, a, b] = keep.tile([P, PASS], U8, name="plane_%s_%d_%d" % (name, a, b), tag=tag, bufs=bufs, align_bytes=64)
            width = PASS // pieces
            for first in range(0, PASS, width):
                nc.vector.quantize_mx(out=codes[name, a, b][:, first:first + width].bitcast(FP8X4), scales=planes[name, a, b][:, first:first + width],
                                      in_=rounded[name, a, b][:, PACK * first:PACK * (first + width)])

        sines, products = {}, {}
        sums = [keep.tile([P, PACK, S], F32, name="sums%d" % b) for b in range(H_PASSES)]

        def inbound_sines(b):
            sines[b] = keep.tile([P, PACK, S], F32, name="sines")
            for t in range(PACK):
                acc = bank(PACK * b + t, "inbound")
                for a in range(K_PASSES):
                    nc.tensor.matmul_mx(out=acc[:], lhsT=codes["w1", a, b][:, t * P:(t + 1) * P].bitcast(FP8X4), lhsT_scale=planes["w1", a, b][:, t * P:(t + 1) * P],
                                        rhs=picked_words[INBOUND][a][:].bitcast(FP8X4), rhs_scale=picked_scales[INBOUND][4 * a:P, :],
                                        start=(a == 0), stop=(a == K_PASSES - 1))
                nc.scalar.activation(out=sines[b][:, t, :], in_=acc[:], func=ACT.Sin)

        def door_sums(b):
            products[b] = keep.tile([P, PACK, S], F32, name="products")
            doors = []
            for t in range(PACK):
                acc = bank(PACK + t, "door")
                for a in range(K_PASSES):
                    column = a * H + b * PASS + t * P
                    nc.tensor.matmul_mx(out=acc[:], lhsT=w2_codes[:, 2 * column:2 * (column + P)].bitcast(FP4X4), lhsT_scale=w2_planes[:, column:column + P],
                                        rhs=picked_words[DOOR][a][:].bitcast(FP8X4), rhs_scale=(picked_scales[DOOR], door_scales_pass1)[a][:],
                                        start=(a == 0), stop=(a == K_PASSES - 1))
                doors.append(acc)
            for first, last in ((0, 1), (1, 2), (2, 4)):
                nc.vector.tensor_tensor(out=products[b][:, first:last, :], in0=sines[b][:, first:last, :], in1=congestion[b][:, first:last, :], op=ALU.mult)
            for t in range(PACK):
                nc.vector.tensor_tensor(out=sums[b][:, t, :], in0=doors[t][:], in1=products[b][:, t, :], op=ALU.add)

        def outbound_pass(accs, a, b):
            for c in range(CHUNKS):
                entries = slice(c * CHUNK, (c + 1) * CHUNK)
                for t in range(PACK):
                    nc.tensor.matmul_mx(out=accs[c][:, t * CHUNK:(t + 1) * CHUNK], lhsT=codes["w3", a, b][:, t * P:(t + 1) * P].bitcast(FP8X4),
                                        lhsT_scale=planes["w3", a, b][:, t * P:(t + 1) * P],
                                        rhs=picked_words[OUTBOUND][a][:, entries].bitcast(FP8X4), rhs_scale=picked_scales[OUTBOUND][4 * a:P, entries],
                                        start=(a == 0 and t == 0), stop=(a == K_PASSES - 1 and t == PACK - 1))

        h_rounded = {}
        h_codes = [mx_tile(S, U32, "h_codes%d" % b) for b in range(H_PASSES)]
        h_planes = [mx_tile(S, U8, "h_plane%d" % b) for b in range(H_PASSES)]

        def larger_side(accs, b, c):
            nc.vector.tensor_tensor(out=h_rounded[b][:, PACK * c * CHUNK:PACK * (c + 1) * CHUNK].rearrange("p (n i t) -> p n t i", i=2, t=PACK),
                                    in0=accs[c][:].rearrange("p (t n i) -> p n t i", i=2, t=PACK),
                                    in1=sums[b][:, :, c * CHUNK:(c + 1) * CHUNK].rearrange("p t (n i) -> p n t i", i=2), op=ALU.max)

        def quantise_h(b, first, last):
            nc.vector.quantize_mx(out=h_codes[b][:, first:last].bitcast(FP8X4), scales=h_planes[b][:, first:last], in_=h_rounded[b][:, PACK * first:PACK * last])

        def score_pass(targets, b, c):
            entries = slice(c * CHUNK, (c + 1) * CHUNK)
            for acc, tiles in targets:
                for place, nt in enumerate(tiles):
                    nc.tensor.matmul_mx(out=acc[:, place * CHUNK:(place + 1) * CHUNK], lhsT=w4_codes[:, b * N + nt * P:b * N + (nt + 1) * P].bitcast(FP8X4),
                                        lhsT_scale=w4_planes[4 * b:P, nt * P:(nt + 1) * P],
                                        rhs=h_codes[b][:, entries].bitcast(FP8X4), rhs_scale=h_planes[b][:, entries],
                                        start=(b == 0 and place == 0), stop=(b == H_PASSES - 1 and place == len(tiles) - 1))

        def store_scores(acc, tiles, c, copy, queue):
            result = ring.tile([P, len(tiles), CHUNK], F32, name="result", bufs=5)
            copy(out=result[:].rearrange("p nt j -> p (nt j)"), in_=acc[:, :len(tiles) * CHUNK])
            queue.dma_start(out=out[tiles[0] * P:(tiles[-1] + 1) * P, c * CHUNK:(c + 1) * CHUNK].rearrange("(nt p) j -> p nt j", p=P), in_=result[:])

        gather_scales(picked_scales[DOOR], table_scales, DOOR)
        nc.sync.dma_start(out=door_scales_pass1[0:P - 4, :].bitcast(I32), in_=picked_scales[DOOR][4:P, :].bitcast(I32))
        load_weight("w3", w3, 1, 0)
        load_weight("w1", w1, 0, 1)
        load_weight("w1", w1, 1, 1)
        load_weight("w3", w3, 0, 1)
        load_congestion(1)
        load_stacked_planes(w4_planes, w4_scales)
        load_weight("w3", w3, 1, 1)
        load_words(w4_codes, w4_words.rearrange("a p c i -> a p (c i)"))
        gather_words(INBOUND, 0)
        gather_words(DOOR, 0)
        gather_words(OUTBOUND, 0)
        gather_scales(picked_scales[INBOUND], table_scales, INBOUND)
        gather_scales(picked_scales[OUTBOUND], table_scales, OUTBOUND)
        deal(nc.scalar.copy, w2_codes[:].bitcast(U16), w2_words_raw[:].bitcast(U16))
        deal(nc.vector.tensor_copy, w2_planes[:], w2_scales_raw[:])
        round_weight("w1", 0, 0, on_scalar)
        quantise_weight("w1", 0, 0, 1)
        round_weight("w1", 1, 0, on_scalar)
        quantise_weight("w1", 1, 0, 1)
        gather_words(INBOUND, 1)
        inbound_sines(0)
        late_words = keep.tile([P, 2 * S], U32, name="late_words", tag="rounded_w1_1_0", align_bytes=64)
        picked_words[DOOR].append(late_words[:, :S])
        picked_words[OUTBOUND].append(late_words[:, S:])
        gather_words(DOOR, 1)
        gather_words(OUTBOUND, 1)
        round_weight("w3", 0, 0, on_scalar)
        quantise_weight("w3", 0, 0, 1)
        outbound = [bank(c, "outbound") for c in range(CHUNKS)]
        outbound_pass(outbound, 0, 0)
        round_weight("w3", 1, 0, on_scalar)
        quantise_weight("w3", 1, 0, 1)
        outbound_pass(outbound, 1, 0)
        door_sums(0)
        round_weight("w1", 0, 1, on_scalar)
        round_weight("w3", 0, 1, on_scalar)
        round_weight("w1", 1, 1, on_vector)
        quantise_weight("w1", 1, 1, 1)
        quantise_weight("w1", 0, 1, 1)
        inbound_sines(1)
        h_rounded[0] = keep.tile([P, PACK * S], BF16, name="h_rounded0", tag="first", align_bytes=64)
        for c in range(CHUNKS):
            larger_side(outbound, 0, c)
        quantise_h(0, 0, S)
        quantise_weight("w3", 0, 1, 1)
        outbound = [bank(c, "outbound") for c in range(CHUNKS)]
        outbound_pass(outbound, 0, 1)
        door_sums(1)
        round_weight("w3", 1, 1, on_scalar)
        quantise_weight("w3", 1, 1, 2)
        outbound_pass(outbound, 1, 1)
        h_rounded[1] = mx_tile(PACK * S, BF16, "h_rounded1")
        every = list(range(N_TILES))
        targets = [[(bank(CHUNKS + c, "scores"), every)] for c in range(CHUNKS)]
        for c in range(CHUNKS):
            score_pass(targets[c], 0, c)
        larger_side(outbound, 1, 0)
        for c in range(CHUNKS):
            if c + 1 < CHUNKS:
                larger_side(outbound, 1, c + 1)
            quantise_h(1, c * CHUNK, (c + 1) * CHUNK)
            score_pass(targets[c], 1, c)
            store_scores(targets[c][0][0], every, c, nc.scalar.copy, nc.sync)
